import numpy as np
import ml_dtypes


def mxq(x, axis, fmt="e4m3"):
    dtype, down = {"e4m3": (ml_dtypes.float8_e4m3fn, 7), "e5m2": (ml_dtypes.float8_e5m2, 14)}[fmt]
    v = np.moveaxis(np.asarray(x, np.float32).astype(ml_dtypes.bfloat16).astype(np.float64), axis, -1)
    blocks = v.reshape(v.shape[:-1] + (-1, 32))
    amax = np.abs(blocks).max(-1, keepdims=True)
    byte = np.maximum(np.where(amax > 0, np.frexp(amax)[1] - 1 + 127, 0) - down, 1)
    scale = np.exp2(byte - 127.0)
    codes = (blocks / scale).astype(np.float32).astype(dtype).astype(np.float64)
    return np.moveaxis((codes * scale).reshape(v.shape), -1, axis)


WIDE = False


def mx_kscale(k):
    if not WIDE:
        return np.ones(k)
    levels = np.array([10, -10, 5, -5, 0])
    if k % 512:
        return np.exp2(np.random.permutation(np.resize(levels, k // 32))).repeat(32)
    a = np.empty((k // 512, 16))
    for p in range(k // 512):
        a[p, :8] = np.random.permutation(np.resize(levels, 8))
        for g in range(8):
            far = levels[np.abs(levels - a[p, g]) >= 10]
            a[p, g + 8] = far[np.random.randint(len(far))]
    return np.exp2(a.ravel()).repeat(32)


def f64(x):
    return np.asarray(x).astype(np.float64)


def striped(idx):
    return np.tile(idx.reshape(-1, 16).T, (8, 1)).astype(np.uint16)


def unstriped(offs):
    return offs[:16].T.reshape(-1).astype(np.int64)


def striped8(idx):
    return np.concatenate([x.reshape(-1, 16).T for x in idx]).astype(np.uint16)


def runs(offs, k):
    lists = np.stack([offs[16 * r : 16 * r + 16].T.reshape(-1) for r in range(8)]).astype(np.int64)
    return lists[np.arange(k) % 512 // 64]


def pack_weight(w):
    k, n = w.shape
    w = f64(np.asarray(w, np.float32).astype(ml_dtypes.bfloat16)).reshape(k // 32, 32, n)
    amax = np.abs(w).max(1)
    byte = np.clip(np.where(amax > 0, np.frexp(amax)[1] - 1 + 127 - 7, 1), 1, 254)
    scaled = (w * np.exp2(127.0 - byte)[:, None, :]).reshape(k, n).astype(np.float32)
    words = np.ascontiguousarray(scaled.reshape(k // 512, 128, 4, n).transpose(0, 1, 3, 2)).astype(ml_dtypes.float8_e4m3fn).view(np.uint8)
    return words, np.ascontiguousarray(byte.astype(np.uint8).reshape(k // 512, 16, n))


def unpack_weight(words, scales):
    g, p, n, _ = words.shape
    vals = np.ascontiguousarray(words).view(ml_dtypes.float8_e4m3fn).astype(np.float64) * np.repeat(np.exp2(scales.astype(np.float64) - 127.0), 8, axis=1)[..., None]
    return vals.transpose(0, 1, 3, 2).reshape(g * 512, n)


E2M1 = np.array([0.0, 0.5, 1.0, 1.5, 2.0, 3.0, 4.0, 6.0, -0.0, -0.5, -1.0, -1.5, -2.0, -3.0, -4.0, -6.0])


def pack_fp4(w):
    k, n = w.shape
    w = f64(np.asarray(w, np.float32).astype(ml_dtypes.bfloat16)).reshape(k // 32, 32, n)
    amax = np.abs(w).max(1)
    mant, ex = np.frexp(amax / 6.0)
    byte = np.clip(np.where(amax > 0, np.where(mant > 0.5, ex, ex - 1) + 127, 1), 1, 254)
    scaled = (w * np.exp2(127.0 - byte)[:, None, :]).reshape(k, n).astype(np.float32)
    c = np.ascontiguousarray(scaled.reshape(k // 512, 128, 4, n).transpose(0, 1, 3, 2)).astype(ml_dtypes.float4_e2m1fn).view(np.uint8) & 0xF
    words = (c[..., 0::2] | (c[..., 1::2] << 4)).reshape(k // 512, 128, 2 * n)
    return np.ascontiguousarray(words), np.ascontiguousarray(byte.astype(np.uint8).reshape(k // 512, 16, n))


def unpack_fp4(words, scales):
    g, _, n = scales.shape
    words = np.ascontiguousarray(words).reshape(g, 128, n, 2)
    nib = np.empty((g, 128, n, 4), np.uint8)
    nib[..., 0::2] = words & 0xF
    nib[..., 1::2] = words >> 4
    vals = E2M1[nib] * np.repeat(np.exp2(scales.astype(np.float64) - 127.0), 8, axis=1)[..., None]
    return vals.transpose(0, 1, 3, 2).reshape(g * 512, n)


def planes(y):
    n, m = y.shape
    v = y.astype(np.float32).astype(ml_dtypes.bfloat16).astype(np.float64).reshape(n // 32, 32, m)
    top = np.abs(v).max(1)
    byte = np.clip(np.where(top > 0, np.frexp(top)[1] - 1 + 127 - 7, 1), 1, 254)
    codes = (v * np.exp2(127.0 - byte)[:, None, :]).reshape(n, m).astype(np.float32).astype(ml_dtypes.float8_e4m3fn).view(np.uint8)
    words = codes.reshape(n // 512, 128, 4, m).transpose(0, 1, 3, 2)
    return np.ascontiguousarray(words), np.ascontiguousarray(byte.astype(np.uint8).reshape(n // 512, 16, m))


K, T, S, N, H = 512, 2048, 512, 512, 512


def setup_inputs():
    n = np.random.standard_normal
    s = mx_kscale(K)[:, None]
    u = mx_kscale(H)
    packed_xT = pack_weight(n((K, T)) * s)
    packed_w1 = pack_fp4(n((K, H)) / np.sqrt(K) / s)
    packed_w2 = pack_fp4(n((H, N)) / np.sqrt(H) / u[:, None])
    packed_w3 = pack_fp4(n((H, N)) / np.sqrt(H) / u[:, None])
    return {
        "x_words": packed_xT[0],
        "x_scales": packed_xT[1],
        "w1_words": packed_w1[0],
        "w1_scales": packed_w1[1],
        "gn": (np.random.uniform(0.5, 1.5, (H, 1)) * u[:, None]).astype(np.float32),
        "w2_words": packed_w2[0],
        "w2_scales": packed_w2[1],
        "gm": (np.random.uniform(0.5, 1.5, (H, 1)) * u[:, None]).astype(np.float32),
        "w3_words": packed_w3[0],
        "w3_scales": packed_w3[1],
        "offs": striped(np.random.permutation(T)[:S]),
        "n1": striped8(np.stack([np.random.permutation(S) for _ in range(8)])),
        "n2": striped8(np.stack([np.random.permutation(S) for _ in range(8)])),
        "n3": striped8(np.stack([np.random.permutation(S) for _ in range(8)])),
        "n4": striped8(np.stack([np.random.permutation(S) for _ in range(8)])),
        "n5": striped8(np.stack([np.random.permutation(S) for _ in range(8)])),
        "n6": striped8(np.stack([np.random.permutation(S) for _ in range(8)])),
        "n7": striped8(np.stack([np.random.permutation(S) for _ in range(8)])),
        "n8": striped8(np.stack([np.random.permutation(S) for _ in range(8)])),
    }


def reference(x_words, x_scales, w1_words, w1_scales, gn, w2_words, w2_scales, gm, w3_words, w3_scales, offs, n1, n2, n3, n4, n5, n6, n7, n8):
    xq = unpack_weight(x_words, x_scales)[:, unstriped(offs)]
    y = unpack_fp4(w1_words, w1_scales).T @ xq
    z = f64(gn) * (np.maximum(y[np.arange(H)[:, None], runs(n1, H)], y[np.arange(H)[:, None], runs(n2, H)]) - (0.75 * y))
    a = unpack_fp4(w2_words, w2_scales).T @ mxq(z, 0, "e4m3")
    z2 = f64(gm) * ((np.tanh(y[np.arange(H)[:, None], runs(n3, H)] - y)) * (y[np.arange(H)[:, None], runs(n4, H)]))
    b = unpack_fp4(w3_words, w3_scales).T @ mxq(z2, 0, "e4m3")
    out_0 = np.maximum(a[np.arange(N)[:, None], runs(n5, N)] + b[np.arange(N)[:, None], runs(n7, N)], a[np.arange(N)[:, None], runs(n6, N)] + b[np.arange(N)[:, None], runs(n8, N)])
    return (out_0,) + planes(out_0)

@@ -1,0 +1,238 @@
+from contextlib import ExitStack
+
+import concourse.mybir as mybir
+
+F32 = mybir.dt.float32
+BF16 = mybir.dt.bfloat16
+I32 = mybir.dt.int32
+U32 = mybir.dt.uint32
+U16 = mybir.dt.uint16
+U8 = mybir.dt.uint8
+FP8X4 = mybir.dt.float8_e4m3fn_x4
+FP4X4 = mybir.dt.float4_e2m1fn_x4
+ALU = mybir.AluOpType
+ACT = mybir.ActivationFunctionType
+
+P = 128
+R = 4
+T = 2048
+S = 512
+C = 256
+FLOPS = 3 * 2 * 512 * 512 * 512
+
+
+def tile_picked_forkpathboverfdif_none_po_kernel(
+    tc, x_words, x_scales, w1_words, w1_scales, gn, w2_words, w2_scales, gm, w3_words, w3_scales,
+    offs, n1, n2, n3, n4, n5, n6, n7, n8, out_0, out_1, out_2,
+):
+    nc = tc.nc
+    with ExitStack() as ctx:
+        keep = ctx.enter_context(tc.tile_pool(name="keep", bufs=1))
+        psum = ctx.enter_context(tc.psum_pool(name="psum", bufs=8))
+
+        def tile(name, shape, dtype):
+            return keep.tile(shape, dtype, name=name, align_bytes=64)
+
+        def load_list(name, src):
+            dst = tile(name, [P, S // 16], U16)
+            nc.sync.dma_start(dst[:], src)
+            return dst
+
+        def load_words(name, src):
+            dst = tile(name, [P, 2 * S], U8)
+            nc.sync.dma_start(dst[:].bitcast(I32), src[0].bitcast(I32))
+            return dst
+
+        def load_scale_rows(dst, src, queues):
+            for q in range(4):
+                queues[q].dma_start(dst[32 * q : 32 * q + 4].bitcast(I32), src[0, 4 * q : 4 * q + 4, :].bitcast(I32))
+
+        def deal_words(name, raw):
+            dst = tile(name, [P, 2 * S], U8)
+            nc.scalar.copy(
+                out=dst[:].bitcast(U16).rearrange("p (t c i) -> p c t i", t=R, i=8),
+                in_=raw[:].bitcast(U16).rearrange("p (c i t) -> p c t i", t=R, i=8),
+            )
+            return dst
+
+        def deal_scales(name, raw, count):
+            dst = tile(name, [P, count * S], U8)
+            nc.vector.tensor_copy(
+                out=dst[:].rearrange("p (w t c i) -> p w c t i", w=count, t=R, i=16),
+                in_=raw[:].rearrange("p (w c i t) -> p w c t i", w=count, t=R, i=16),
+            )
+            return dst
+
+        def cols(h):
+            return slice(h * C, (h + 1) * C)
+
+        def entries(lst, h):
+            return lst[:, h * C // 16 : (h + 1) * C // 16]
+
+        def woven(packed):
+            return packed[:].rearrange("p (c i t) -> p c t i", t=R, i=4)
+
+        def planar(rows):
+            return rows[:].rearrange("p t (c i) -> p c t i", i=4)
+
+        def product(words, scales, t, codes, code_scales):
+            acc = psum.tile([P, C], F32, name="acc")
+            nc.tensor.matmul_mx(
+                out=acc[:],
+                lhsT=words[:, 2 * P * t : 2 * P * (t + 1)].bitcast(FP4X4),
+                lhsT_scale=scales[:, P * t : P * (t + 1)],
+                rhs=codes.bitcast(FP8X4),
+                rhs_scale=code_scales,
+                start=True,
+                stop=True,
+            )
+            return acc
+
+        xs_raw = tile("xs_raw", [P, T], U8)
+        w1s_raw = tile("w1s_raw", [P, S], U8)
+        w23s_raw = tile("w23s_raw", [P, 2 * S], U8)
+        nc.vector.memset(xs_raw[:].bitcast(I32), 0)
+        nc.gpsimd.memset(w1s_raw[:].bitcast(I32), 0)
+        nc.gpsimd.memset(w23s_raw[:].bitcast(I32), 0)
+
+        offs_t = load_list("offs_t", offs)
+        w1w_raw = load_words("w1w_raw", w1_words)
+        xw_raw = tile("xw_raw", [P, T], I32)
+        nc.sync.dma_start(xw_raw[:], x_words[0].rearrange("p n r -> p (n r)").bitcast(I32))
+        load_scale_rows(xs_raw[:], x_scales, [nc.scalar] * 4)
+        load_scale_rows(w1s_raw[:], w1_scales, [nc.scalar, nc.scalar, nc.gpsimd, nc.gpsimd])
+        w3w_raw = load_words("w3w_raw", w3_words)
+        l3 = load_list("l3", n3)
+        l4 = load_list("l4", n4)
+        l1 = load_list("l1", n1)
+        l2 = load_list("l2", n2)
+        w2w_raw = load_words("w2w_raw", w2_words)
+        gm_t = tile("gm_t", [P, R], F32)
+        nc.sync.dma_start(gm_t[:], gm.rearrange("(p t) o -> p (t o)", t=R))
+        gn_t = tile("gn_t", [P, R], F32)
+        nc.sync.dma_start(gn_t[:], gn.rearrange("(p t) o -> p (t o)", t=R))
+        load_scale_rows(w23s_raw[:, S:], w3_scales, [nc.sync] * 4)
+        load_scale_rows(w23s_raw[:, :S], w2_scales, [nc.sync] * 4)
+        l7 = load_list("l7", n7)
+        l8 = load_list("l8", n8)
+        l5 = load_list("l5", n5)
+        l6 = load_list("l6", n6)
+
+        w1w = deal_words("w1w", w1w_raw)
+        w1s = deal_scales("w1s", w1s_raw, 1)
+        xs = tile("xs", [P, S], U8)
+        nc.vector.tensor_copy(xs[:], xs_raw[:].indirect(offs_t[:]))
+        y = [tile("y%d" % t, [P, S], F32) for t in range(R)]
+        for h in range(2):
+            xw = tile("xw%d" % h, [P, C], U32)
+            nc.vector.tensor_copy(xw[:], xw_raw[:].bitcast(U32).indirect(entries(offs_t, h)))
+            for t in range(R):
+                acc = product(w1w, w1s, t, xw[:], xs[:, cols(h)])
+                if h == 1 and t % 2 == 1:
+                    nc.vector.tensor_copy(y[t][:, cols(h)], acc[:])
+                else:
+                    nc.scalar.activation(y[t][:, cols(h)], acc[:], ACT.Copy)
+        w3w = deal_words("w3w", w3w_raw)
+        w2w = deal_words("w2w", w2w_raw)
+
+        def quantise(name, rows, gain):
+            packed = tile(name + "_bf", [P, C * R], BF16)
+            nc.vector.tensor_tensor(
+                woven(packed), planar(rows), gain[:].unsqueeze(1).unsqueeze(3).to_broadcast([P, C // 4, R, 4]), ALU.mult
+            )
+            codes = tile(name + "_codes", [P, C], U32)
+            scales = tile(name + "_scales", [P, C], U8)
+            return packed, codes, scales
+
+        def run_quantise(packed, codes, scales):
+            nc.vector.quantize_mx(out=codes[:].bitcast(FP8X4), scales=scales[:], in_=packed[:])
+
+        def layer(words, scales, codes, code_scales, dst, h):
+            for t in range(R):
+                acc = product(words, scales, t, codes[:], code_scales[:])
+                nc.scalar.activation(dst[t][:, cols(h)], acc[:], ACT.Copy)
+
+        th = []
+        g3 = [tile("g3_%d" % h, [P, R, C], F32) for h in range(2)]
+        for t in range(R):
+            nc.vector.tensor_copy(g3[0][:, t, :], y[t][:].indirect(entries(l3, 0)))
+            nc.scalar.activation(g3[1][:, t, :], y[t][:].indirect(entries(l3, 1)), ACT.Copy)
+        w23s = deal_scales("w23s", w23s_raw, 2)
+        for h in range(2):
+            d = tile("d%d" % h, [P, R, C], F32)
+            th.append(tile("th%d" % h, [P, R, C], F32))
+            for t in range(R):
+                nc.vector.tensor_tensor(d[:, t, :], g3[h][:, t, :], y[t][:, cols(h)], ALU.subtract)
+                if t % 2 == 1:
+                    nc.scalar.activation(th[h][:, t - 1 : t + 1, :], d[:, t - 1 : t + 1, :], ACT.Tanh)
+        b = [tile("b%d" % t, [P, S], F32) for t in range(R)]
+        a = [tile("a%d" % t, [P, S], F32) for t in range(R)]
+        g1 = [tile("g1_%d" % h, [P, R, C], F32) for h in range(2)]
+        g2 = [tile("g2_%d" % h, [P, R, C], F32) for h in range(2)]
+        q2 = []
+        for h in range(2):
+            p2 = tile("p2_%d" % h, [P, R, C], F32)
+            for t in range(R):
+                nc.vector.tensor_tensor(p2[:, t, :], y[t][:].indirect(entries(l4, h)), th[h][:, t, :], ALU.mult)
+            if h == 1:
+                run_quantise(*q2[0])
+            q2.append(quantise("z2_%d" % h, p2, gm_t))
+        for h in range(2):
+            for t in range(R):
+                nc.scalar.activation(g1[h][:, t, :], y[t][:].indirect(entries(l1, h)), ACT.Copy)
+                nc.scalar.activation(g2[h][:, t, :], y[t][:].indirect(entries(l2, h)), ACT.Copy)
+            if h == 0:
+                layer(w3w, w23s[:, S:], q2[0][1], q2[0][2], b, 0)
+
+        q1 = []
+        for h in range(2):
+            m = tile("m%d" % h, [P, R, C], F32)
+            nc.vector.tensor_tensor(m[:], g1[h][:], g2[h][:], ALU.max)
+            if h == 0:
+                run_quantise(*q2[1])
+                layer(w3w, w23s[:, S:], q2[1][1], q2[1][2], b, 1)
+            else:
+                run_quantise(*q1[0])
+                layer(w2w, w23s[:, :S], q1[0][1], q1[0][2], a, 0)
+            e = tile("e%d" % h, [P, R, C], F32)
+            for t in range(R):
+                nc.vector.scalar_tensor_tensor(e[:, t, :], y[t][:, cols(h)], -0.75, m[:, t, :], ALU.mult, ALU.add)
+            q1.append(quantise("z_%d" % h, e, gn_t))
+        run_quantise(*q1[1])
+        layer(w2w, w23s[:, :S], q1[1][1], q1[1][2], a, 1)
+
+        out_rows = out_0.rearrange("(p t) j -> p t j", t=R)
+        out_words = out_1[0].rearrange("p n r -> p (n r)").bitcast(I32)
+        o_scales = tile("o_scales", [P, S], U8)
+        for h in range(2):
+            g7 = []
+            g8 = []
+            for t in range(R):
+                g7.append(tile("g7_%d" % t, [P, C], F32))
+                g8.append(tile("g8_%d" % t, [P, C], F32))
+                if h == 0 and t == R - 1:
+                    nc.vector.tensor_copy(g7[t][:], b[t][:].indirect(entries(l7, h)))
+                else:
+                    nc.scalar.activation(g7[t][:], b[t][:].indirect(entries(l7, h)), ACT.Copy)
+                nc.scalar.activation(g8[t][:], b[t][:].indirect(entries(l8, h)), ACT.Copy)
+            s1 = tile("s1_%d" % h, [P, R, C], F32)
+            s2 = tile("s2_%d" % h, [P, R, C], F32)
+            o = tile("o%d" % h, [P, R, C], F32)
+            for t in range(R):
+                nc.vector.tensor_tensor(s1[:, t, :], a[t][:].indirect(entries(l5, h)), g7[t][:], ALU.add)
+                if t > 0:
+                    nc.vector.tensor_tensor(o[:, t - 1, :], s1[:, t - 1, :], s2[:, t - 1, :], ALU.max)
+                nc.vector.tensor_tensor(s2[:, t, :], a[t][:].indirect(entries(l6, h)), g8[t][:], ALU.add)
+            nc.vector.tensor_tensor(o[:, R - 1, :], s1[:, R - 1, :], s2[:, R - 1, :], ALU.max)
+            nc.sync.dma_start(out_rows[:, :, cols(h)], o[:])
+            o_bf = tile("o_bf%d" % h, [P, C * R], BF16)
+            if h == 0:
+                nc.scalar.copy(woven(o_bf), planar(o))
+            else:
+                nc.vector.tensor_copy(woven(o_bf), planar(o))
+            o_codes = tile("o_codes%d" % h, [P, C], U32)
+            nc.vector.quantize_mx(out=o_codes[:].bitcast(FP8X4), scales=o_scales[:, cols(h)], in_=o_bf[:])
+            nc.sync.dma_start(out_words[:, cols(h)], o_codes[:].bitcast(I32))
+        for q in range(4):
+            queue = nc.scalar if q % 2 == 0 else nc.sync
+            queue.dma_start(out_2[0, 4 * q : 4 * q + 4, :].bitcast(I32), o_scales[32 * q : 32 * q + 4, :].bitcast(I32))

@@ -18,6 +18,11 @@ R = 4
 T = 2048
 S = 512
 C = 256
+FILL = 0
+FUSED_N4 = (0,1)
+PLAIN_N6 = (2,3)
+PLAIN_N3 = 2
+BUBBLE = 3
 FLOPS = 3 * 2 * 512 * 512 * 512
 
 
@@ -90,29 +95,29 @@ def tile_picked_forkpathboverfdif_none_po_kernel(
 
         xs_raw = tile("xs_raw", [P, T], U8)
         w1s_raw = tile("w1s_raw", [P, S], U8)
-        w23s_raw = tile("w23s_raw", [P, 2 * S], U8)
-        nc.vector.memset(xs_raw[:].bitcast(I32), 0)
-        nc.gpsimd.memset(w1s_raw[:].bitcast(I32), 0)
-        nc.gpsimd.memset(w23s_raw[:].bitcast(I32), 0)
+        w2s_raw = tile("w2s_raw", [P, S], U8)
+        w3s_raw = tile("w3s_raw", [P, S], U8)
+        for raw in (xs_raw, w1s_raw, w3s_raw, w2s_raw):
+            nc.vector.memset(raw[:].bitcast(I32), 0)
 
         offs_t = load_list("offs_t", offs)
         w1w_raw = load_words("w1w_raw", w1_words)
         xw_raw = tile("xw_raw", [P, T], I32)
         nc.sync.dma_start(xw_raw[:], x_words[0].rearrange("p n r -> p (n r)").bitcast(I32))
         load_scale_rows(xs_raw[:], x_scales, [nc.scalar] * 4)
-        load_scale_rows(w1s_raw[:], w1_scales, [nc.scalar, nc.scalar, nc.gpsimd, nc.gpsimd])
-        w3w_raw = load_words("w3w_raw", w3_words)
+        load_scale_rows(w1s_raw[:], w1_scales, [nc.scalar, nc.scalar, nc.scalar, nc.gpsimd])
         l3 = load_list("l3", n3)
         l4 = load_list("l4", n4)
         l1 = load_list("l1", n1)
         l2 = load_list("l2", n2)
+        load_scale_rows(w3s_raw[:], w3_scales, [nc.gpsimd] * 4)
+        load_scale_rows(w2s_raw[:], w2_scales, [nc.gpsimd] * 4)
+        w3w_raw = load_words("w3w_raw", w3_words)
         w2w_raw = load_words("w2w_raw", w2_words)
         gm_t = tile("gm_t", [P, R], F32)
         nc.sync.dma_start(gm_t[:], gm.rearrange("(p t) o -> p (t o)", t=R))
         gn_t = tile("gn_t", [P, R], F32)
         nc.sync.dma_start(gn_t[:], gn.rearrange("(p t) o -> p (t o)", t=R))
-        load_scale_rows(w23s_raw[:, S:], w3_scales, [nc.sync] * 4)
-        load_scale_rows(w23s_raw[:, :S], w2_scales, [nc.sync] * 4)
         l7 = load_list("l7", n7)
         l8 = load_list("l8", n8)
         l5 = load_list("l5", n5)
@@ -123,113 +128,145 @@ def tile_picked_forkpathboverfdif_none_po_kernel(
         xs = tile("xs", [P, S], U8)
         nc.vector.tensor_copy(xs[:], xs_raw[:].indirect(offs_t[:]))
         y = [tile("y%d" % t, [P, S], F32) for t in range(R)]
+        yc = [tile("yc%d" % h, [P, R, C], F32) for h in range(2)]
+        xw = [tile("xw%d" % h, [P, C], U32) for h in range(2)]
         for h in range(2):
-            xw = tile("xw%d" % h, [P, C], U32)
-            nc.vector.tensor_copy(xw[:], xw_raw[:].bitcast(U32).indirect(entries(offs_t, h)))
-            for t in range(R):
-                acc = product(w1w, w1s, t, xw[:], xs[:, cols(h)])
-                if h == 1 and t % 2 == 1:
+            nc.vector.tensor_copy(xw[h][:], xw_raw[:].bitcast(U32).indirect(entries(offs_t, h)))
+        for t in range(R):
+            for h in range(2):
+                acc = product(w1w, w1s, t, xw[h][:], xs[:, cols(h)])
+                if h == 1 and t in (1, 3):
                     nc.vector.tensor_copy(y[t][:, cols(h)], acc[:])
                 else:
                     nc.scalar.activation(y[t][:, cols(h)], acc[:], ACT.Copy)
-        w3w = deal_words("w3w", w3w_raw)
-        w2w = deal_words("w2w", w2w_raw)
+        pieces = [(h, t) for h in range(2) for t in range(R)]
+        for h, t in pieces[PLAIN_N3:] + pieces[:PLAIN_N3]:
+            nc.sync.dma_start(yc[h][:, t, :], y[t][:, cols(h)])
 
-        def quantise(name, rows, gain):
+        def weave(name, rows, engine="vector"):
             packed = tile(name + "_bf", [P, C * R], BF16)
-            nc.vector.tensor_tensor(
-                woven(packed), planar(rows), gain[:].unsqueeze(1).unsqueeze(3).to_broadcast([P, C // 4, R, 4]), ALU.mult
-            )
+            if engine == "vector":
+                nc.vector.tensor_copy(woven(packed), planar(rows))
+            else:
+                nc.scalar.copy(woven(packed), planar(rows))
+            return packed
+
+        def weave_times(name, rows, gain):
+            packed = tile(name + "_bf", [P, C * R], BF16)
+            spread = gain[:].unsqueeze(1).unsqueeze(3).to_broadcast([P, C // 4, R, 4])
+            nc.vector.tensor_tensor(woven(packed), planar(rows), spread, ALU.mult)
+            return packed
+
+        def quantise(name, packed):
             codes = tile(name + "_codes", [P, C], U32)
             scales = tile(name + "_scales", [P, C], U8)
-            return packed, codes, scales
-
-        def run_quantise(packed, codes, scales):
             nc.vector.quantize_mx(out=codes[:].bitcast(FP8X4), scales=scales[:], in_=packed[:])
+            return codes, scales
+
+        def fetch(engine, dst, window, lst, h):
+            if engine == "vector":
+                nc.vector.tensor_copy(dst, window[:].indirect(entries(lst, h)))
+            else:
+                nc.scalar.activation(dst, window[:].indirect(entries(lst, h)), ACT.Copy)
 
         def layer(words, scales, codes, code_scales, dst, h):
             for t in range(R):
                 acc = product(words, scales, t, codes[:], code_scales[:])
                 nc.scalar.activation(dst[t][:, cols(h)], acc[:], ACT.Copy)
 
-        th = []
-        g3 = [tile("g3_%d" % h, [P, R, C], F32) for h in range(2)]
-        for t in range(R):
-            nc.vector.tensor_copy(g3[0][:, t, :], y[t][:].indirect(entries(l3, 0)))
-            nc.scalar.activation(g3[1][:, t, :], y[t][:].indirect(entries(l3, 1)), ACT.Copy)
-        w23s = deal_scales("w23s", w23s_raw, 2)
-        for h in range(2):
-            d = tile("d%d" % h, [P, R, C], F32)
-            th.append(tile("th%d" % h, [P, R, C], F32))
-            for t in range(R):
-                nc.vector.tensor_tensor(d[:, t, :], g3[h][:, t, :], y[t][:, cols(h)], ALU.subtract)
-                if t % 2 == 1:
-                    nc.scalar.activation(th[h][:, t - 1 : t + 1, :], d[:, t - 1 : t + 1, :], ACT.Tanh)
         b = [tile("b%d" % t, [P, S], F32) for t in range(R)]
         a = [tile("a%d" % t, [P, S], F32) for t in range(R)]
         g1 = [tile("g1_%d" % h, [P, R, C], F32) for h in range(2)]
         g2 = [tile("g2_%d" % h, [P, R, C], F32) for h in range(2)]
-        q2 = []
+        g4 = [tile("g4_%d" % h, [P, R, C], F32) for h in range(2)]
+        th = [tile("th%d" % h, [P, R, C], F32) for h in range(2)]
+        p2 = [tile("p2_%d" % h, [P, R, C], F32) for h in range(2)]
+        g3 = tile("g3", [P, R, C], F32)
+        for t in range(PLAIN_N3):
+            fetch("vector", g3[:, t, :], y[t], l3, 0)
+        for t in range(FILL):
+            fetch("vector", g1[0][:, t, :], y[t], l1, 0)
         for h in range(2):
-            p2 = tile("p2_%d" % h, [P, R, C], F32)
+            if not FUSED_N4[h]:
+                for t in range(R):
+                    fetch("scalar", g4[h][:, t, :], y[t], l4, h)
+            d = tile("d%d" % h, [P, R, C], F32)
             for t in range(R):
-                nc.vector.tensor_tensor(p2[:, t, :], y[t][:].indirect(entries(l4, h)), th[h][:, t, :], ALU.mult)
-            if h == 1:
-                run_quantise(*q2[0])
-            q2.append(quantise("z2_%d" % h, p2, gm_t))
+                if h == 0 and t < PLAIN_N3:
+                    nc.vector.tensor_tensor(d[:, t, :], g3[:, t, :], y[t][:, cols(h)], ALU.subtract)
+                else:
+                    nc.vector.tensor_tensor(d[:, t, :], y[t][:].indirect(entries(l3, h)), yc[h][:, t, :], ALU.subtract)
+                if t % 2 == 1:
+                    nc.scalar.activation(th[h][:, t - 1 : t + 1, :], d[:, t - 1 : t + 1, :], ACT.Tanh)
+        w3w = deal_words("w3w", w3w_raw)
+        w3s = deal_scales("w3s", w3s_raw, 1)
+        z2_bf = []
         for h in range(2):
             for t in range(R):
-                nc.scalar.activation(g1[h][:, t, :], y[t][:].indirect(entries(l1, h)), ACT.Copy)
-                nc.scalar.activation(g2[h][:, t, :], y[t][:].indirect(entries(l2, h)), ACT.Copy)
+                if FUSED_N4[h]:
+                    nc.vector.tensor_tensor(p2[h][:, t, :], y[t][:].indirect(entries(l4, h)), th[h][:, t, :], ALU.mult)
+                else:
+                    nc.vector.scalar_tensor_tensor(p2[h][:, t, :], th[h][:, t, :], gm_t[:, t : t + 1], g4[h][:, t, :], ALU.mult, ALU.mult)
+                if h == 1 and t == 1:
+                    z2_q0 = quantise("z2_0", z2_bf[0])
+            if FUSED_N4[h]:
+                z2_bf.append(weave_times("z2_%d" % h, p2[h], gm_t))
+            else:
+                z2_bf.append(weave("z2_%d" % h, p2[h], ["vector","vector"][h]))
+        for h in range(2):
+            for t in range(R):
+                if h == 1 or t >= FILL:
+                    fetch("scalar", g1[h][:, t, :], y[t], l1, h)
+                fetch("scalar", g2[h][:, t, :], y[t], l2, h)
             if h == 0:
-                layer(w3w, w23s[:, S:], q2[0][1], q2[0][2], b, 0)
+                layer(w3w, w3s, z2_q0[0], z2_q0[1], b, 0)
+        w2w = deal_words("w2w", w2w_raw)
 
-        q1 = []
+        z_bf = []
         for h in range(2):
             m = tile("m%d" % h, [P, R, C], F32)
             nc.vector.tensor_tensor(m[:], g1[h][:], g2[h][:], ALU.max)
             if h == 0:
-                run_quantise(*q2[1])
-                layer(w3w, w23s[:, S:], q2[1][1], q2[1][2], b, 1)
+                z2_q1 = quantise("z2_1", z2_bf[1])
+                layer(w3w, w3s, z2_q1[0], z2_q1[1], b, 1)
             else:
-                run_quantise(*q1[0])
-                layer(w2w, w23s[:, :S], q1[0][1], q1[0][2], a, 0)
+                z_q0 = quantise("z_0", z_bf[0])
+                layer(w2w, w2s, z_q0[0], z_q0[1], a, 0)
             e = tile("e%d" % h, [P, R, C], F32)
-            for t in range(R):
-                nc.vector.scalar_tensor_tensor(e[:, t, :], y[t][:, cols(h)], -0.75, m[:, t, :], ALU.mult, ALU.add)
-            q1.append(quantise("z_%d" % h, e, gn_t))
-        run_quantise(*q1[1])
-        layer(w2w, w23s[:, :S], q1[1][1], q1[1][2], a, 1)
+            nc.vector.scalar_tensor_tensor(e[:], yc[h][:], -0.75, m[:], ALU.mult, ALU.add)
+            if h == 0:
+                w2s = deal_scales("w2s", w2s_raw, 1)
+            z_bf.append(weave_times("z_%d" % h, e, gn_t))
+        z_q1 = quantise("z_1", z_bf[1])
+        layer(w2w, w2s, z_q1[0], z_q1[1], a, 1)
 
         out_rows = out_0.rearrange("(p t) j -> p t j", t=R)
         out_words = out_1[0].rearrange("p n r -> p (n r)").bitcast(I32)
         o_scales = tile("o_scales", [P, S], U8)
         for h in range(2):
-            g7 = []
-            g8 = []
+            g7 = [tile("g7_%d" % t, [P, C], F32) for t in range(R)]
+            g8 = [tile("g8_%d" % t, [P, C], F32) for t in range(R)]
+            g6 = tile("g6_%d" % h, [P, R, C], F32)
             for t in range(R):
-                g7.append(tile("g7_%d" % t, [P, C], F32))
-                g8.append(tile("g8_%d" % t, [P, C], F32))
-                if h == 0 and t == R - 1:
-                    nc.vector.tensor_copy(g7[t][:], b[t][:].indirect(entries(l7, h)))
-                else:
-                    nc.scalar.activation(g7[t][:], b[t][:].indirect(entries(l7, h)), ACT.Copy)
-                nc.scalar.activation(g8[t][:], b[t][:].indirect(entries(l8, h)), ACT.Copy)
+                fetch("vector" if h == 0 and t >= R - BUBBLE else "scalar", g7[t][:], b[t], l7, h)
+                fetch("scalar", g8[t][:], b[t], l8, h)
+            for t in range(R - PLAIN_N6[h], R):
+                fetch("scalar", g6[:, t, :], a[t], l6, h)
             s1 = tile("s1_%d" % h, [P, R, C], F32)
             s2 = tile("s2_%d" % h, [P, R, C], F32)
             o = tile("o%d" % h, [P, R, C], F32)
             for t in range(R):
                 nc.vector.tensor_tensor(s1[:, t, :], a[t][:].indirect(entries(l5, h)), g7[t][:], ALU.add)
-                if t > 0:
-                    nc.vector.tensor_tensor(o[:, t - 1, :], s1[:, t - 1, :], s2[:, t - 1, :], ALU.max)
-                nc.vector.tensor_tensor(s2[:, t, :], a[t][:].indirect(entries(l6, h)), g8[t][:], ALU.add)
-            nc.vector.tensor_tensor(o[:, R - 1, :], s1[:, R - 1, :], s2[:, R - 1, :], ALU.max)
-            nc.sync.dma_start(out_rows[:, :, cols(h)], o[:])
-            o_bf = tile("o_bf%d" % h, [P, C * R], BF16)
-            if h == 0:
-                nc.scalar.copy(woven(o_bf), planar(o))
-            else:
-                nc.vector.tensor_copy(woven(o_bf), planar(o))
+                if t == 2:
+                    nc.vector.tensor_tensor(o[:, :2, :], s1[:, :2, :], s2[:, :2, :], ALU.max)
+                    nc.sync.dma_start(out_rows[:, :2, cols(h)], o[:, :2, :])
+                if t >= R - PLAIN_N6[h]:
+                    nc.vector.tensor_tensor(s2[:, t, :], g6[:, t, :], g8[t][:], ALU.add)
+                else:
+                    nc.vector.tensor_tensor(s2[:, t, :], a[t][:].indirect(entries(l6, h)), g8[t][:], ALU.add)
+            nc.vector.tensor_tensor(o[:, 2:, :], s1[:, 2:, :], s2[:, 2:, :], ALU.max)
+            nc.sync.dma_start(out_rows[:, 2:, cols(h)], o[:, 2:, :])
+            o_bf = weave("o%d" % h, o, "scalar" if h == 0 else "vector")
             o_codes = tile("o_codes%d" % h, [P, C], U32)
             nc.vector.quantize_mx(out=o_codes[:].bitcast(FP8X4), scales=o_scales[:, cols(h)], in_=o_bf[:])
             nc.sync.dma_start(out_words[:, cols(h)], o_codes[:].bitcast(I32))

@@ -18,11 +18,10 @@ R = 4
 T = 2048
 S = 512
 C = 256
-FILL = 0
-FUSED_N4 = (0,1)
-PLAIN_N6 = (2,3)
-PLAIN_N3 = 2
-BUBBLE = 3
+PLAIN_N6 = (2,2)
+COPIED = 0
+PLAIN_N5 = (0, 0)
+BUBBLE = 2
 FLOPS = 3 * 2 * 512 * 512 * 512
 
 
@@ -48,9 +47,14 @@ def tile_picked_forkpathboverfdif_none_po_kernel(
             nc.sync.dma_start(dst[:].bitcast(I32), src[0].bitcast(I32))
             return dst
 
+        def load_gain(name, src):
+            dst = tile(name, [P, R], F32)
+            nc.sync.dma_start(dst[:], src.rearrange("(p t) o -> p (t o)", t=R))
+            return dst
+
         def load_scale_rows(dst, src, queues):
             for q in range(4):
-                queues[q].dma_start(dst[32 * q : 32 * q + 4].bitcast(I32), src[0, 4 * q : 4 * q + 4, :].bitcast(I32))
+                queues[q].dma_start(dst[32 * q : 32 * q + 4, :].bitcast(I32), src[0, 4 * q : 4 * q + 4, :].bitcast(I32))
 
         def deal_words(name, raw):
             dst = tile(name, [P, 2 * S], U8)
@@ -60,28 +64,28 @@ def tile_picked_forkpathboverfdif_none_po_kernel(
             )
             return dst
 
-        def deal_scales(name, raw, count):
-            dst = tile(name, [P, count * S], U8)
+        def deal_scales(name, raw):
+            dst = tile(name, [P, S], U8)
             nc.vector.tensor_copy(
-                out=dst[:].rearrange("p (w t c i) -> p w c t i", w=count, t=R, i=16),
-                in_=raw[:].rearrange("p (w c i t) -> p w c t i", w=count, t=R, i=16),
+                out=dst[:].rearrange("p (t c i) -> p c t i", t=R, i=16),
+                in_=raw[:].rearrange("p (c i t) -> p c t i", t=R, i=16),
             )
             return dst
 
         def cols(h):
             return slice(h * C, (h + 1) * C)
 
-        def entries(lst, h):
-            return lst[:, h * C // 16 : (h + 1) * C // 16]
+        def looked_up(window, lst, h):
+            return window[:].indirect(lst[:, h * C // 16 : (h + 1) * C // 16])
 
         def woven(packed):
             return packed[:].rearrange("p (c i t) -> p c t i", t=R, i=4)
 
         def planar(rows):
-            return rows[:].rearrange("p t (c i) -> p c t i", i=4)
+            return rows.rearrange("p t (c i) -> p c t i", i=4)
 
-        def product(words, scales, t, codes, code_scales):
-            acc = psum.tile([P, C], F32, name="acc")
+        def product(words, scales, t, codes, code_scales, width=C):
+            acc = psum.tile([P, width], F32, name="acc")
             nc.tensor.matmul_mx(
                 out=acc[:],
                 lhsT=words[:, 2 * P * t : 2 * P * (t + 1)].bitcast(FP4X4),
@@ -93,56 +97,6 @@ def tile_picked_forkpathboverfdif_none_po_kernel(
             )
             return acc
 
-        xs_raw = tile("xs_raw", [P, T], U8)
-        w1s_raw = tile("w1s_raw", [P, S], U8)
-        w2s_raw = tile("w2s_raw", [P, S], U8)
-        w3s_raw = tile("w3s_raw", [P, S], U8)
-        for raw in (xs_raw, w1s_raw, w3s_raw, w2s_raw):
-            nc.vector.memset(raw[:].bitcast(I32), 0)
-
-        offs_t = load_list("offs_t", offs)
-        w1w_raw = load_words("w1w_raw", w1_words)
-        xw_raw = tile("xw_raw", [P, T], I32)
-        nc.sync.dma_start(xw_raw[:], x_words[0].rearrange("p n r -> p (n r)").bitcast(I32))
-        load_scale_rows(xs_raw[:], x_scales, [nc.scalar] * 4)
-        load_scale_rows(w1s_raw[:], w1_scales, [nc.scalar, nc.scalar, nc.scalar, nc.gpsimd])
-        l3 = load_list("l3", n3)
-        l4 = load_list("l4", n4)
-        l1 = load_list("l1", n1)
-        l2 = load_list("l2", n2)
-        load_scale_rows(w3s_raw[:], w3_scales, [nc.gpsimd] * 4)
-        load_scale_rows(w2s_raw[:], w2_scales, [nc.gpsimd] * 4)
-        w3w_raw = load_words("w3w_raw", w3_words)
-        w2w_raw = load_words("w2w_raw", w2_words)
-        gm_t = tile("gm_t", [P, R], F32)
-        nc.sync.dma_start(gm_t[:], gm.rearrange("(p t) o -> p (t o)", t=R))
-        gn_t = tile("gn_t", [P, R], F32)
-        nc.sync.dma_start(gn_t[:], gn.rearrange("(p t) o -> p (t o)", t=R))
-        l7 = load_list("l7", n7)
-        l8 = load_list("l8", n8)
-        l5 = load_list("l5", n5)
-        l6 = load_list("l6", n6)
-
-        w1w = deal_words("w1w", w1w_raw)
-        w1s = deal_scales("w1s", w1s_raw, 1)
-        xs = tile("xs", [P, S], U8)
-        nc.vector.tensor_copy(xs[:], xs_raw[:].indirect(offs_t[:]))
-        y = [tile("y%d" % t, [P, S], F32) for t in range(R)]
-        yc = [tile("yc%d" % h, [P, R, C], F32) for h in range(2)]
-        xw = [tile("xw%d" % h, [P, C], U32) for h in range(2)]
-        for h in range(2):
-            nc.vector.tensor_copy(xw[h][:], xw_raw[:].bitcast(U32).indirect(entries(offs_t, h)))
-        for t in range(R):
-            for h in range(2):
-                acc = product(w1w, w1s, t, xw[h][:], xs[:, cols(h)])
-                if h == 1 and t in (1, 3):
-                    nc.vector.tensor_copy(y[t][:, cols(h)], acc[:])
-                else:
-                    nc.scalar.activation(y[t][:, cols(h)], acc[:], ACT.Copy)
-        pieces = [(h, t) for h in range(2) for t in range(R)]
-        for h, t in pieces[PLAIN_N3:] + pieces[:PLAIN_N3]:
-            nc.sync.dma_start(yc[h][:, t, :], y[t][:, cols(h)])
-
         def weave(name, rows, engine="vector"):
             packed = tile(name + "_bf", [P, C * R], BF16)
             if engine == "vector":
@@ -151,94 +105,120 @@ def tile_picked_forkpathboverfdif_none_po_kernel(
                 nc.scalar.copy(woven(packed), planar(rows))
             return packed
 
-        def weave_times(name, rows, gain):
-            packed = tile(name + "_bf", [P, C * R], BF16)
-            spread = gain[:].unsqueeze(1).unsqueeze(3).to_broadcast([P, C // 4, R, 4])
+        def weave_times(name, rows, gain, width):
+            packed = tile(name + "_bf", [P, width * R], BF16)
+            spread = gain[:].unsqueeze(1).unsqueeze(3).to_broadcast([P, width // 4, R, 4])
             nc.vector.tensor_tensor(woven(packed), planar(rows), spread, ALU.mult)
             return packed
 
-        def quantise(name, packed):
-            codes = tile(name + "_codes", [P, C], U32)
-            scales = tile(name + "_scales", [P, C], U8)
+        def quantise(name, packed, width):
+            codes = tile(name + "_codes", [P, width], U32)
+            scales = tile(name + "_scales", [P, width], U8)
             nc.vector.quantize_mx(out=codes[:].bitcast(FP8X4), scales=scales[:], in_=packed[:])
             return codes, scales
 
         def fetch(engine, dst, window, lst, h):
             if engine == "vector":
-                nc.vector.tensor_copy(dst, window[:].indirect(entries(lst, h)))
+                nc.vector.tensor_copy(dst, looked_up(window, lst, h))
             else:
-                nc.scalar.activation(dst, window[:].indirect(entries(lst, h)), ACT.Copy)
+                nc.scalar.activation(dst, looked_up(window, lst, h), ACT.Copy)
 
-        def layer(words, scales, codes, code_scales, dst, h):
+        def layer(words, scales, quantised, dst, h):
             for t in range(R):
-                acc = product(words, scales, t, codes[:], code_scales[:])
+                acc = product(words, scales, t, quantised[0][:], quantised[1][:])
                 nc.scalar.activation(dst[t][:, cols(h)], acc[:], ACT.Copy)
+
+        xs_raw = tile("xs_raw", [P, T], U8)
+        w1s_raw = tile("xw1", [P, S], U8)
+        w3s_raw = tile("w3s_raw", [P, S], U8)
+        w2s_raw = tile("w2s_raw", [P, S], U8)
+        y = [tile("y%d" % t, [P, 2 * S], F32) for t in range(R)]
+        for raw in (xs_raw, w1s_raw, w3s_raw, w2s_raw):
+            nc.gpsimd.memset(raw[:].bitcast(I32), 0)
+
+        offs_t = load_list("offs_t", offs)
+        w1w_raw = load_words("w1w_raw", w1_words)
+        load_scale_rows(xs_raw, x_scales, [nc.sync] * 4)
+        xw_raw = tile("xw_raw", [P, T], I32)
+        nc.sync.dma_start(xw_raw[:], x_words[0].rearrange("p n r -> p (n r)").bitcast(I32))
+        load_scale_rows(w1s_raw, w1_scales, [nc.sync] * 4)
+        l3 = load_list("l3", n3)
+        l1 = load_list("l1", n1)
+        l4 = load_list("l4", n4)
+        l2 = load_list("l2", n2)
+        gm_t = load_gain("gm_t", gm)
+        w3w_raw = load_words("w3w_raw", w3_words)
+        load_scale_rows(w3s_raw, w3_scales, [nc.sync] * 4)
+        gn_t = load_gain("gn_t", gn)
+        w2w_raw = load_words("w2w_raw", w2_words)
+        load_scale_rows(w2s_raw, w2_scales, [nc.sync] * 4)
+        l7 = load_list("l7", n7)
+        l8 = load_list("l8", n8)
+        l5 = load_list("l5", n5)
+        l6 = load_list("l6", n6)
+
+        w1w = deal_words("w1w", w1w_raw)
+        w1s = deal_scales("w1s", w1s_raw)
+        xs = tile("xs", [P, S], U8)
+        nc.vector.tensor_copy(xs[:], xs_raw[:].indirect(offs_t[:]))
+        xw = [tile("xw%d" % h, [P, C], U32) for h in range(2)]
+        for h in range(2):
+            nc.vector.tensor_copy(xw[h][:], looked_up(xw_raw[:].bitcast(U32), offs_t, h))
+        for t in range(R):
+            for h in range(2):
+                acc = product(w1w, w1s, t, xw[h][:], xs[:, cols(h)])
+                if h == 1 and t in (1, 3):
+                    nc.vector.tensor_copy(y[t][:, cols(h)], acc[:])
+                else:
+                    nc.scalar.activation(y[t][:, cols(h)], acc[:], ACT.Copy)
+
+        def rows(name, width=C):
+            return tile(name, [P, R, width], F32)
+
+        def fetch_row(engine, dst, window, lst):
+            if engine == "vector":
+                nc.vector.tensor_copy(dst, window[:].indirect(lst[:]))
+            else:
+                nc.scalar.activation(dst, window[:].indirect(lst[:]), ACT.Copy)
+
+        def fetch_with(dst, window, lst, other, op):
+            nc.vector.tensor_tensor(dst, window[:].indirect(lst[:]), other, op)
 
         b = [tile("b%d" % t, [P, S], F32) for t in range(R)]
         a = [tile("a%d" % t, [P, S], F32) for t in range(R)]
-        g1 = [tile("g1_%d" % h, [P, R, C], F32) for h in range(2)]
-        g2 = [tile("g2_%d" % h, [P, R, C], F32) for h in range(2)]
-        g4 = [tile("g4_%d" % h, [P, R, C], F32) for h in range(2)]
-        th = [tile("th%d" % h, [P, R, C], F32) for h in range(2)]
-        p2 = [tile("p2_%d" % h, [P, R, C], F32) for h in range(2)]
-        g3 = tile("g3", [P, R, C], F32)
-        for t in range(PLAIN_N3):
-            fetch("vector", g3[:, t, :], y[t], l3, 0)
-        for t in range(FILL):
-            fetch("vector", g1[0][:, t, :], y[t], l1, 0)
-        for h in range(2):
-            if not FUSED_N4[h]:
-                for t in range(R):
-                    fetch("scalar", g4[h][:, t, :], y[t], l4, h)
-            d = tile("d%d" % h, [P, R, C], F32)
-            for t in range(R):
-                if h == 0 and t < PLAIN_N3:
-                    nc.vector.tensor_tensor(d[:, t, :], g3[:, t, :], y[t][:, cols(h)], ALU.subtract)
-                else:
-                    nc.vector.tensor_tensor(d[:, t, :], y[t][:].indirect(entries(l3, h)), yc[h][:, t, :], ALU.subtract)
-                if t % 2 == 1:
-                    nc.scalar.activation(th[h][:, t - 1 : t + 1, :], d[:, t - 1 : t + 1, :], ACT.Tanh)
+        g1, g2, g3, d, th, p2, e = [rows(name, S) for name in ("g1", "g2", "g3", "d", "th", "p2", "e")]
+        for t in range(R - COPIED):
+            fetch_row("scalar" if t >= R - COPIED - 2 else "vector", g3[:, t, :], y[t], l3)
+        for t in range(R):
+            if t < R - COPIED:
+                nc.vector.tensor_tensor(d[:, t, :], g3[:, t, :], y[t][:, :S], ALU.subtract)
+            nc.scalar.activation(th[:, t, :], d[:, t, :], ACT.Tanh)
+        for t in range(R):
+            fetch_with(p2[:, t, :], y[t], l4, th[:, t, :], ALU.mult)
         w3w = deal_words("w3w", w3w_raw)
-        w3s = deal_scales("w3s", w3s_raw, 1)
-        z2_bf = []
-        for h in range(2):
-            for t in range(R):
-                if FUSED_N4[h]:
-                    nc.vector.tensor_tensor(p2[h][:, t, :], y[t][:].indirect(entries(l4, h)), th[h][:, t, :], ALU.mult)
-                else:
-                    nc.vector.scalar_tensor_tensor(p2[h][:, t, :], th[h][:, t, :], gm_t[:, t : t + 1], g4[h][:, t, :], ALU.mult, ALU.mult)
-                if h == 1 and t == 1:
-                    z2_q0 = quantise("z2_0", z2_bf[0])
-            if FUSED_N4[h]:
-                z2_bf.append(weave_times("z2_%d" % h, p2[h], gm_t))
-            else:
-                z2_bf.append(weave("z2_%d" % h, p2[h], ["vector","vector"][h]))
-        for h in range(2):
-            for t in range(R):
-                if h == 1 or t >= FILL:
-                    fetch("scalar", g1[h][:, t, :], y[t], l1, h)
-                fetch("scalar", g2[h][:, t, :], y[t], l2, h)
-            if h == 0:
-                layer(w3w, w3s, z2_q0[0], z2_q0[1], b, 0)
+        z2_bf = weave_times("z2", p2[:], gm_t, S)
+        w3s = deal_scales("w3s", w3s_raw)
+        z2_codes, z2_scales = quantise("z2", z2_bf, S)
+        for t in range(R):
+            fetch_row("scalar", g1[:, t, :], y[t], l1)
+            fetch_row("scalar", g2[:, t, :], y[t], l2)
+        for t in range(R):
+            acc = product(w3w, w3s, t, z2_codes[:], z2_scales[:], S)
+            nc.scalar.activation(b[t][:], acc[:], ACT.Copy)
         w2w = deal_words("w2w", w2w_raw)
 
-        z_bf = []
-        for h in range(2):
-            m = tile("m%d" % h, [P, R, C], F32)
-            nc.vector.tensor_tensor(m[:], g1[h][:], g2[h][:], ALU.max)
-            if h == 0:
-                z2_q1 = quantise("z2_1", z2_bf[1])
-                layer(w3w, w3s, z2_q1[0], z2_q1[1], b, 1)
-            else:
-                z_q0 = quantise("z_0", z_bf[0])
-                layer(w2w, w2s, z_q0[0], z_q0[1], a, 0)
-            e = tile("e%d" % h, [P, R, C], F32)
-            nc.vector.scalar_tensor_tensor(e[:], yc[h][:], -0.75, m[:], ALU.mult, ALU.add)
-            if h == 0:
-                w2s = deal_scales("w2s", w2s_raw, 1)
-            z_bf.append(weave_times("z_%d" % h, e, gn_t))
-        z_q1 = quantise("z_1", z_bf[1])
-        layer(w2w, w2s, z_q1[0], z_q1[1], a, 1)
+        m = p2
+        for t in range(R + 1):
+            if t < R:
+                nc.vector.tensor_tensor(m[:, t, :], g1[:, t, :], g2[:, t, :], ALU.max)
+            if t > 0:
+                nc.vector.scalar_tensor_tensor(e[:, t - 1, :], y[t - 1][:, :S], -0.75, m[:, t - 1, :], ALU.mult, ALU.add)
+        z_bf = weave_times("z", e[:], gn_t, S)
+        w2s = deal_scales("w2s", w2s_raw)
+        z_codes, z_scales = quantise("z", z_bf, S)
+        for t in range(R):
+            acc = product(w2w, w2s, t, z_codes[:], z_scales[:], S)
+            nc.scalar.activation(a[t][:], acc[:], ACT.Copy)
 
         out_rows = out_0.rearrange("(p t) j -> p t j", t=R)
         out_words = out_1[0].rearrange("p n r -> p (n r)").bitcast(I32)
@@ -246,27 +226,32 @@ def tile_picked_forkpathboverfdif_none_po_kernel(
         for h in range(2):
             g7 = [tile("g7_%d" % t, [P, C], F32) for t in range(R)]
             g8 = [tile("g8_%d" % t, [P, C], F32) for t in range(R)]
-            g6 = tile("g6_%d" % h, [P, R, C], F32)
+            g6 = rows("g6_%d" % h)
             for t in range(R):
                 fetch("vector" if h == 0 and t >= R - BUBBLE else "scalar", g7[t][:], b[t], l7, h)
                 fetch("scalar", g8[t][:], b[t], l8, h)
-            for t in range(R - PLAIN_N6[h], R):
-                fetch("scalar", g6[:, t, :], a[t], l6, h)
-            s1 = tile("s1_%d" % h, [P, R, C], F32)
-            s2 = tile("s2_%d" % h, [P, R, C], F32)
-            o = tile("o%d" % h, [P, R, C], F32)
             for t in range(R):
-                nc.vector.tensor_tensor(s1[:, t, :], a[t][:].indirect(entries(l5, h)), g7[t][:], ALU.add)
-                if t == 2:
-                    nc.vector.tensor_tensor(o[:, :2, :], s1[:, :2, :], s2[:, :2, :], ALU.max)
-                    nc.sync.dma_start(out_rows[:, :2, cols(h)], o[:, :2, :])
+                if t >= R - PLAIN_N6[h]:
+                    fetch("scalar", g6[:, t, :], a[t], l6, h)
+            s1 = rows("s1_%d" % h)
+            s2 = rows("s2_%d" % h)
+            o = rows("o%d" % h)
+
+            def larger(first, last):
+                nc.vector.tensor_tensor(o[:, first:last, :], s1[:, first:last, :], s2[:, first:last, :], ALU.max)
+                nc.sync.dma_start(out_rows[:, first:last, cols(h)], o[:, first:last, :])
+
+            for t in range(R):
+                if True:
+                    nc.vector.tensor_tensor(s1[:, t, :], looked_up(a[t], l5, h), g7[t][:], ALU.add)
+                if t == 3:
+                    larger(0, 3)
                 if t >= R - PLAIN_N6[h]:
                     nc.vector.tensor_tensor(s2[:, t, :], g6[:, t, :], g8[t][:], ALU.add)
                 else:
-                    nc.vector.tensor_tensor(s2[:, t, :], a[t][:].indirect(entries(l6, h)), g8[t][:], ALU.add)
-            nc.vector.tensor_tensor(o[:, 2:, :], s1[:, 2:, :], s2[:, 2:, :], ALU.max)
-            nc.sync.dma_start(out_rows[:, 2:, cols(h)], o[:, 2:, :])
-            o_bf = weave("o%d" % h, o, "scalar" if h == 0 else "vector")
+                    nc.vector.tensor_tensor(s2[:, t, :], looked_up(a[t], l6, h), g8[t][:], ALU.add)
+            larger(3, R)
+            o_bf = weave("o%d" % h, o[:], "scalar" if h == 0 else "vector")
             o_codes = tile("o_codes%d" % h, [P, C], U32)
             nc.vector.quantize_mx(out=o_codes[:].bitcast(FP8X4), scales=o_scales[:, cols(h)], in_=o_bf[:])
             nc.sync.dma_start(out_words[:, cols(h)], o_codes[:].bitcast(I32))

@@ -20,8 +20,9 @@ S = 512
 C = 256
 PLAIN_N6 = (2,2)
 COPIED = 0
-PLAIN_N5 = (0, 0)
-BUBBLE = 2
+PLAIN_N5 = (0, 1)
+AHEAD = 0
+BUBBLE = 1
 FLOPS = 3 * 2 * 512 * 512 * 512
 
 
@@ -69,6 +70,14 @@ def tile_picked_forkpathboverfdif_none_po_kernel(
             nc.vector.tensor_copy(
                 out=dst[:].rearrange("p (t c i) -> p c t i", t=R, i=16),
                 in_=raw[:].rearrange("p (c i t) -> p c t i", t=R, i=16),
+            )
+            return dst
+
+        def deal_bytes(name, raw, width):
+            dst = tile(name, [P, width * S], U8)
+            nc.gpsimd.tensor_copy(
+                out=dst[:].rearrange("p (t m b) -> p t m b", t=R, b=width),
+                in_=raw[:].rearrange("p (m t b) -> p t m b", t=R, b=width),
             )
             return dst
 
@@ -129,7 +138,7 @@ def tile_picked_forkpathboverfdif_none_po_kernel(
                 nc.scalar.activation(dst[t][:, cols(h)], acc[:], ACT.Copy)
 
         xs_raw = tile("xs_raw", [P, T], U8)
-        w1s_raw = tile("xw1", [P, S], U8)
+        w1s_raw = tile("w1s_raw", [P, S], U8)
         w3s_raw = tile("w3s_raw", [P, S], U8)
         w2s_raw = tile("w2s_raw", [P, S], U8)
         y = [tile("y%d" % t, [P, 2 * S], F32) for t in range(R)]
@@ -144,21 +153,21 @@ def tile_picked_forkpathboverfdif_none_po_kernel(
         load_scale_rows(w1s_raw, w1_scales, [nc.sync] * 4)
         l3 = load_list("l3", n3)
         l1 = load_list("l1", n1)
+        w3w_raw = load_words("w3w_raw", w3_words)
+        w2w_raw = load_words("w2w_raw", w2_words)
         l4 = load_list("l4", n4)
         l2 = load_list("l2", n2)
-        gm_t = load_gain("gm_t", gm)
-        w3w_raw = load_words("w3w_raw", w3_words)
         load_scale_rows(w3s_raw, w3_scales, [nc.sync] * 4)
-        gn_t = load_gain("gn_t", gn)
-        w2w_raw = load_words("w2w_raw", w2_words)
         load_scale_rows(w2s_raw, w2_scales, [nc.sync] * 4)
+        gm_t = load_gain("gm_t", gm)
+        gn_t = load_gain("gn_t", gn)
         l7 = load_list("l7", n7)
         l8 = load_list("l8", n8)
         l5 = load_list("l5", n5)
         l6 = load_list("l6", n6)
 
         w1w = deal_words("w1w", w1w_raw)
-        w1s = deal_scales("w1s", w1s_raw)
+        w1s = deal_bytes("w1s", w1s_raw, 1)
         xs = tile("xs", [P, S], U8)
         nc.vector.tensor_copy(xs[:], xs_raw[:].indirect(offs_t[:]))
         xw = [tile("xw%d" % h, [P, C], U32) for h in range(2)]
@@ -195,9 +204,9 @@ def tile_picked_forkpathboverfdif_none_po_kernel(
             nc.scalar.activation(th[:, t, :], d[:, t, :], ACT.Tanh)
         for t in range(R):
             fetch_with(p2[:, t, :], y[t], l4, th[:, t, :], ALU.mult)
-        w3w = deal_words("w3w", w3w_raw)
+        w3w = deal_bytes("w3w", w3w_raw, 2)
         z2_bf = weave_times("z2", p2[:], gm_t, S)
-        w3s = deal_scales("w3s", w3s_raw)
+        w3s = deal_bytes("w3s", w3s_raw, 1)
         z2_codes, z2_scales = quantise("z2", z2_bf, S)
         for t in range(R):
             fetch_row("scalar", g1[:, t, :], y[t], l1)
@@ -205,7 +214,7 @@ def tile_picked_forkpathboverfdif_none_po_kernel(
         for t in range(R):
             acc = product(w3w, w3s, t, z2_codes[:], z2_scales[:], S)
             nc.scalar.activation(b[t][:], acc[:], ACT.Copy)
-        w2w = deal_words("w2w", w2w_raw)
+        w2w = deal_bytes("w2w", w2w_raw, 2)
 
         m = p2
         for t in range(R + 1):
@@ -214,23 +223,32 @@ def tile_picked_forkpathboverfdif_none_po_kernel(
             if t > 0:
                 nc.vector.scalar_tensor_tensor(e[:, t - 1, :], y[t - 1][:, :S], -0.75, m[:, t - 1, :], ALU.mult, ALU.add)
         z_bf = weave_times("z", e[:], gn_t, S)
-        w2s = deal_scales("w2s", w2s_raw)
+        w2s = deal_bytes("w2s", w2s_raw, 1)
         z_codes, z_scales = quantise("z", z_bf, S)
         for t in range(R):
             acc = product(w2w, w2s, t, z_codes[:], z_scales[:], S)
-            nc.scalar.activation(a[t][:], acc[:], ACT.Copy)
+            if t < 1:
+                nc.vector.tensor_copy(a[t][:], acc[:])
+            else:
+                nc.scalar.activation(a[t][:], acc[:], ACT.Copy)
 
         out_rows = out_0.rearrange("(p t) j -> p t j", t=R)
         out_words = out_1[0].rearrange("p n r -> p (n r)").bitcast(I32)
         o_scales = tile("o_scales", [P, S], U8)
         for h in range(2):
-            g7 = [tile("g7_%d" % t, [P, C], F32) for t in range(R)]
-            g8 = [tile("g8_%d" % t, [P, C], F32) for t in range(R)]
+            g7 = [tile("g7_%d_%d" % (t, h * (t < AHEAD)), [P, C], F32) if h == 1 or t < R - BUBBLE else None for t in range(R)]
+            if h == 0:
+                late = tile("z_bf", [P, R, C], F32)
+                g7 = [late[:, t, :] if t >= R - BUBBLE else g7[t] for t in range(R)]
+            g8 = [tile("g8_%d_%d" % (t, h * (t < AHEAD)), [P, C], F32) for t in range(R)]
             g6 = rows("g6_%d" % h)
             for t in range(R):
                 fetch("vector" if h == 0 and t >= R - BUBBLE else "scalar", g7[t][:], b[t], l7, h)
                 fetch("scalar", g8[t][:], b[t], l8, h)
+            g5 = rows("g5_%d" % h) if PLAIN_N5[h] else None
             for t in range(R):
+                if t >= R - PLAIN_N5[h]:
+                    fetch("scalar", g5[:, t, :], a[t], l5, h)
                 if t >= R - PLAIN_N6[h]:
                     fetch("scalar", g6[:, t, :], a[t], l6, h)
             s1 = rows("s1_%d" % h)
@@ -242,10 +260,12 @@ def tile_picked_forkpathboverfdif_none_po_kernel(
                 nc.sync.dma_start(out_rows[:, first:last, cols(h)], o[:, first:last, :])
 
             for t in range(R):
-                if True:
+                if t >= R - PLAIN_N5[h]:
+                    nc.vector.tensor_tensor(s1[:, t, :], g5[:, t, :], g7[t][:], ALU.add)
+                else:
                     nc.vector.tensor_tensor(s1[:, t, :], looked_up(a[t], l5, h), g7[t][:], ALU.add)
-                if t == 3:
-                    larger(0, 3)
+                if t >= 2:
+                    larger((0, 2)[t - 2], t)
                 if t >= R - PLAIN_N6[h]:
                     nc.vector.tensor_tensor(s2[:, t, :], g6[:, t, :], g8[t][:], ALU.add)
                 else:

@@ -17,12 +17,14 @@ P = 128
 R = 4
 T = 2048
 S = 512
-C = 256
-PLAIN_N6 = (2,2)
-COPIED = 0
-PLAIN_N5 = (0, 1)
-AHEAD = 0
-BUBBLE = 1
+C = S // 2
+QUADRANTS = 4
+PER_COLUMN = 16
+PSUM_BANKS = 8
+
+VECTOR_N3 = 2
+SCALAR_N6 = 2
+
 FLOPS = 3 * 2 * 512 * 512 * 512
 
 
@@ -33,13 +35,16 @@ def tile_picked_forkpathboverfdif_none_po_kernel(
     nc = tc.nc
     with ExitStack() as ctx:
         keep = ctx.enter_context(tc.tile_pool(name="keep", bufs=1))
-        psum = ctx.enter_context(tc.psum_pool(name="psum", bufs=8))
+        psum = ctx.enter_context(tc.psum_pool(name="psum", bufs=PSUM_BANKS))
 
         def tile(name, shape, dtype):
             return keep.tile(shape, dtype, name=name, align_bytes=64)
 
+        def row_sets(name, width):
+            return tile(name, [P, R, width], F32)
+
         def load_list(name, src):
-            dst = tile(name, [P, S // 16], U16)
+            dst = tile(name, [P, S // PER_COLUMN], U16)
             nc.sync.dma_start(dst[:], src)
             return dst
 
@@ -53,25 +58,9 @@ def tile_picked_forkpathboverfdif_none_po_kernel(
             nc.sync.dma_start(dst[:], src.rearrange("(p t) o -> p (t o)", t=R))
             return dst
 
-        def load_scale_rows(dst, src, queues):
-            for q in range(4):
-                queues[q].dma_start(dst[32 * q : 32 * q + 4, :].bitcast(I32), src[0, 4 * q : 4 * q + 4, :].bitcast(I32))
-
-        def deal_words(name, raw):
-            dst = tile(name, [P, 2 * S], U8)
-            nc.scalar.copy(
-                out=dst[:].bitcast(U16).rearrange("p (t c i) -> p c t i", t=R, i=8),
-                in_=raw[:].bitcast(U16).rearrange("p (c i t) -> p c t i", t=R, i=8),
-            )
-            return dst
-
-        def deal_scales(name, raw):
-            dst = tile(name, [P, S], U8)
-            nc.vector.tensor_copy(
-                out=dst[:].rearrange("p (t c i) -> p c t i", t=R, i=16),
-                in_=raw[:].rearrange("p (c i t) -> p c t i", t=R, i=16),
-            )
-            return dst
+        def load_scale_rows(dst, src):
+            for q in range(QUADRANTS):
+                nc.sync.dma_start(dst[32 * q : 32 * q + 4, :].bitcast(I32), src[0, 4 * q : 4 * q + 4, :].bitcast(I32))
 
         def deal_bytes(name, raw, width):
             dst = tile(name, [P, width * S], U8)
@@ -84,40 +73,19 @@ def tile_picked_forkpathboverfdif_none_po_kernel(
         def cols(h):
             return slice(h * C, (h + 1) * C)
 
-        def looked_up(window, lst, h):
-            return window[:].indirect(lst[:, h * C // 16 : (h + 1) * C // 16])
+        def half_looked_up(window, lst, h):
+            return window[:].indirect(lst[:, h * C // PER_COLUMN : (h + 1) * C // PER_COLUMN])
 
         def woven(packed):
-            return packed[:].rearrange("p (c i t) -> p c t i", t=R, i=4)
+            return packed.rearrange("p (c i t) -> p c t i", t=R, i=4)
 
-        def planar(rows):
-            return rows.rearrange("p t (c i) -> p c t i", i=4)
+        def planar(values):
+            return values.rearrange("p t (c i) -> p c t i", i=4)
 
-        def product(words, scales, t, codes, code_scales, width=C):
-            acc = psum.tile([P, width], F32, name="acc")
-            nc.tensor.matmul_mx(
-                out=acc[:],
-                lhsT=words[:, 2 * P * t : 2 * P * (t + 1)].bitcast(FP4X4),
-                lhsT_scale=scales[:, P * t : P * (t + 1)],
-                rhs=codes.bitcast(FP8X4),
-                rhs_scale=code_scales,
-                start=True,
-                stop=True,
-            )
-            return acc
-
-        def weave(name, rows, engine="vector"):
-            packed = tile(name + "_bf", [P, C * R], BF16)
-            if engine == "vector":
-                nc.vector.tensor_copy(woven(packed), planar(rows))
-            else:
-                nc.scalar.copy(woven(packed), planar(rows))
-            return packed
-
-        def weave_times(name, rows, gain, width):
-            packed = tile(name + "_bf", [P, width * R], BF16)
+        def weave_times(name, values, gain, width):
+            packed = tile(name, [P, width * R], BF16)
             spread = gain[:].unsqueeze(1).unsqueeze(3).to_broadcast([P, width // 4, R, 4])
-            nc.vector.tensor_tensor(woven(packed), planar(rows), spread, ALU.mult)
+            nc.vector.tensor_tensor(woven(packed[:]), planar(values), spread, ALU.mult)
             return packed
 
         def quantise(name, packed, width):
@@ -126,16 +94,22 @@ def tile_picked_forkpathboverfdif_none_po_kernel(
             nc.vector.quantize_mx(out=codes[:].bitcast(FP8X4), scales=scales[:], in_=packed[:])
             return codes, scales
 
-        def fetch(engine, dst, window, lst, h):
-            if engine == "vector":
-                nc.vector.tensor_copy(dst, looked_up(window, lst, h))
-            else:
-                nc.scalar.activation(dst, looked_up(window, lst, h), ACT.Copy)
+        def product(acc, words, scales, t, codes, code_scales):
+            nc.tensor.matmul_mx(
+                out=acc,
+                lhsT=words[:, 2 * P * t : 2 * P * (t + 1)].bitcast(FP4X4),
+                lhsT_scale=scales[:, P * t : P * (t + 1)],
+                rhs=codes.bitcast(FP8X4),
+                rhs_scale=code_scales,
+                start=True,
+                stop=True,
+            )
 
-        def layer(words, scales, quantised, dst, h):
-            for t in range(R):
-                acc = product(words, scales, t, quantised[0][:], quantised[1][:])
-                nc.scalar.activation(dst[t][:, cols(h)], acc[:], ACT.Copy)
+        def move(on_vector, dst, src):
+            if on_vector:
+                nc.vector.tensor_copy(dst, src)
+            else:
+                nc.scalar.activation(dst, src, ACT.Copy)
 
         xs_raw = tile("xs_raw", [P, T], U8)
         w1s_raw = tile("w1s_raw", [P, S], U8)
@@ -147,134 +121,145 @@ def tile_picked_forkpathboverfdif_none_po_kernel(
 
         offs_t = load_list("offs_t", offs)
         w1w_raw = load_words("w1w_raw", w1_words)
-        load_scale_rows(xs_raw, x_scales, [nc.sync] * 4)
+        load_scale_rows(xs_raw, x_scales)
         xw_raw = tile("xw_raw", [P, T], I32)
         nc.sync.dma_start(xw_raw[:], x_words[0].rearrange("p n r -> p (n r)").bitcast(I32))
-        load_scale_rows(w1s_raw, w1_scales, [nc.sync] * 4)
+        load_scale_rows(w1s_raw, w1_scales)
         l3 = load_list("l3", n3)
         l1 = load_list("l1", n1)
         w3w_raw = load_words("w3w_raw", w3_words)
         w2w_raw = load_words("w2w_raw", w2_words)
         l4 = load_list("l4", n4)
         l2 = load_list("l2", n2)
-        load_scale_rows(w3s_raw, w3_scales, [nc.sync] * 4)
-        load_scale_rows(w2s_raw, w2_scales, [nc.sync] * 4)
         gm_t = load_gain("gm_t", gm)
+        load_scale_rows(w3s_raw, w3_scales)
+        load_scale_rows(w2s_raw, w2_scales)
         gn_t = load_gain("gn_t", gn)
         l7 = load_list("l7", n7)
         l8 = load_list("l8", n8)
         l5 = load_list("l5", n5)
         l6 = load_list("l6", n6)
 
-        w1w = deal_words("w1w", w1w_raw)
+        w1w = tile("w1w", [P, 2 * S], U8)
+        nc.scalar.copy(
+            out=w1w[:].bitcast(U16).rearrange("p (t c i) -> p c t i", t=R, i=8),
+            in_=w1w_raw[:].bitcast(U16).rearrange("p (c i t) -> p c t i", t=R, i=8),
+        )
         w1s = deal_bytes("w1s", w1s_raw, 1)
         xs = tile("xs", [P, S], U8)
         nc.vector.tensor_copy(xs[:], xs_raw[:].indirect(offs_t[:]))
         xw = [tile("xw%d" % h, [P, C], U32) for h in range(2)]
         for h in range(2):
-            nc.vector.tensor_copy(xw[h][:], looked_up(xw_raw[:].bitcast(U32), offs_t, h))
+            nc.vector.tensor_copy(xw[h][:], half_looked_up(xw_raw[:].bitcast(U32), offs_t, h))
         for t in range(R):
             for h in range(2):
-                acc = product(w1w, w1s, t, xw[h][:], xs[:, cols(h)])
-                if h == 1 and t in (1, 3):
-                    nc.vector.tensor_copy(y[t][:, cols(h)], acc[:])
-                else:
-                    nc.scalar.activation(y[t][:, cols(h)], acc[:], ACT.Copy)
-
-        def rows(name, width=C):
-            return tile(name, [P, R, width], F32)
-
-        def fetch_row(engine, dst, window, lst):
-            if engine == "vector":
-                nc.vector.tensor_copy(dst, window[:].indirect(lst[:]))
-            else:
-                nc.scalar.activation(dst, window[:].indirect(lst[:]), ACT.Copy)
-
-        def fetch_with(dst, window, lst, other, op):
-            nc.vector.tensor_tensor(dst, window[:].indirect(lst[:]), other, op)
+                acc = psum.tile([P, C], F32, name="acc")
+                product(acc[:], w1w, w1s, t, xw[h][:], xs[:, cols(h)])
+                move(h == 1 and t % 2 == 1, y[t][:, cols(h)], acc[:])
 
         b = [tile("b%d" % t, [P, S], F32) for t in range(R)]
         a = [tile("a%d" % t, [P, S], F32) for t in range(R)]
-        g1, g2, g3, d, th, p2, e = [rows(name, S) for name in ("g1", "g2", "g3", "d", "th", "p2", "e")]
-        for t in range(R - COPIED):
-            fetch_row("scalar" if t >= R - COPIED - 2 else "vector", g3[:, t, :], y[t], l3)
+        y_n1, y_n2, y_n3, diff, th, prod, z_bare = [
+            row_sets(name, S) for name in ("y_n1", "y_n2", "y_n3", "diff", "th", "prod", "z_bare")
+        ]
         for t in range(R):
-            if t < R - COPIED:
-                nc.vector.tensor_tensor(d[:, t, :], g3[:, t, :], y[t][:, :S], ALU.subtract)
-            nc.scalar.activation(th[:, t, :], d[:, t, :], ACT.Tanh)
+            move(t < VECTOR_N3, y_n3[:, t, :], y[t][:].indirect(l3[:]))
         for t in range(R):
-            fetch_with(p2[:, t, :], y[t], l4, th[:, t, :], ALU.mult)
+            nc.vector.tensor_tensor(diff[:, t, :], y_n3[:, t, :], y[t][:, :S], ALU.subtract)
+            nc.scalar.activation(th[:, t, :], diff[:, t, :], ACT.Tanh)
+        for t in range(R):
+            nc.vector.tensor_tensor(prod[:, t, :], y[t][:].indirect(l4[:]), th[:, t, :], ALU.mult)
+        for t in range(R):
+            move(False, y_n1[:, t, :], y[t][:].indirect(l1[:]))
+            move(False, y_n2[:, t, :], y[t][:].indirect(l2[:]))
+
+        top = [th[:, 2, :], th[:, 1, :], prod[:, 2, :], prod[:, 3, :]]
+
+        def larger_neighbour(t):
+            nc.vector.tensor_tensor(top[t], y_n1[:, t, :], y_n2[:, t, :], ALU.max)
+
         w3w = deal_bytes("w3w", w3w_raw, 2)
-        z2_bf = weave_times("z2", p2[:], gm_t, S)
         w3s = deal_bytes("w3s", w3s_raw, 1)
+        larger_neighbour(0)
+        z2_bf = weave_times("z2_bf", prod[:], gm_t, S)
+        larger_neighbour(1)
         z2_codes, z2_scales = quantise("z2", z2_bf, S)
         for t in range(R):
-            fetch_row("scalar", g1[:, t, :], y[t], l1)
-            fetch_row("scalar", g2[:, t, :], y[t], l2)
-        for t in range(R):
-            acc = product(w3w, w3s, t, z2_codes[:], z2_scales[:], S)
-            nc.scalar.activation(b[t][:], acc[:], ACT.Copy)
+            acc = psum.tile([P, S], F32, name="acc")
+            product(acc[:], w3w, w3s, t, z2_codes[:], z2_scales[:])
+            move(False, b[t][:], acc[:])
         w2w = deal_bytes("w2w", w2w_raw, 2)
 
-        m = p2
-        for t in range(R + 1):
-            if t < R:
-                nc.vector.tensor_tensor(m[:, t, :], g1[:, t, :], g2[:, t, :], ALU.max)
-            if t > 0:
-                nc.vector.scalar_tensor_tensor(e[:, t - 1, :], y[t - 1][:, :S], -0.75, m[:, t - 1, :], ALU.mult, ALU.add)
-        z_bf = weave_times("z", e[:], gn_t, S)
-        w2s = deal_bytes("w2s", w2s_raw, 1)
-        z_codes, z_scales = quantise("z", z_bf, S)
         for t in range(R):
-            acc = product(w2w, w2s, t, z_codes[:], z_scales[:], S)
-            if t < 1:
-                nc.vector.tensor_copy(a[t][:], acc[:])
-            else:
-                nc.scalar.activation(a[t][:], acc[:], ACT.Copy)
+            for part in [slice(0, S)] if t < R - 1 else [cols(0), cols(1)]:
+                nc.vector.scalar_tensor_tensor(z_bare[:, t, part], y[t][:, part], -0.75, top[t][:, part], ALU.mult, ALU.add)
+            if t + 2 < R:
+                larger_neighbour(t + 2)
+        w2s = deal_bytes("w2s", w2s_raw, 1)
+        z_bf = [weave_times("z_bf%d" % h, z_bare[:, :, cols(h)], gn_t, C) for h in range(2)]
+        z_q = [quantise("z%d" % h, z_bf[h], C) for h in range(2)]
+        for t in range(R):
+            acc = psum.tile([P, S], F32, name="acc")
+            for h in range(2):
+                product(acc[:, cols(h)], w2w, w2s, t, z_q[h][0][:], z_q[h][1][:])
+            move(t == 0, a[t][:], acc[:])
 
         out_rows = out_0.rearrange("(p t) j -> p t j", t=R)
         out_words = out_1[0].rearrange("p n r -> p (n r)").bitcast(I32)
         o_scales = tile("o_scales", [P, S], U8)
+        last = R - 1
         for h in range(2):
-            g7 = [tile("g7_%d_%d" % (t, h * (t < AHEAD)), [P, C], F32) if h == 1 or t < R - BUBBLE else None for t in range(R)]
-            if h == 0:
-                late = tile("z_bf", [P, R, C], F32)
-                g7 = [late[:, t, :] if t >= R - BUBBLE else g7[t] for t in range(R)]
-            g8 = [tile("g8_%d_%d" % (t, h * (t < AHEAD)), [P, C], F32) for t in range(R)]
-            g6 = rows("g6_%d" % h)
+            b_n7 = [tile("b_n7_%d" % t, [P, C], F32) for t in range(last)]
+            b_n7.append(tile("z_bf0" if h == 0 else "b_n7_last", [P, C], F32))
+            b_n8 = [tile("b_n8_%d" % t, [P, C], F32) for t in range(R)]
             for t in range(R):
-                fetch("vector" if h == 0 and t >= R - BUBBLE else "scalar", g7[t][:], b[t], l7, h)
-                fetch("scalar", g8[t][:], b[t], l8, h)
-            g5 = rows("g5_%d" % h) if PLAIN_N5[h] else None
+                move(h == 0 and t == last, b_n7[t][:], half_looked_up(b[t], l7, h))
+                move(False, b_n8[t][:], half_looked_up(b[t], l8, h))
+            scalar_n5 = [last] if h == 1 else []
+            a_n5 = {t: tile("a_n5", [P, C], F32) for t in scalar_n5}
+            a_n6 = {t: tile("a_n6_%d_%d" % (h, t), [P, C], F32) for t in range(R - SCALAR_N6, R)}
             for t in range(R):
-                if t >= R - PLAIN_N5[h]:
-                    fetch("scalar", g5[:, t, :], a[t], l5, h)
-                if t >= R - PLAIN_N6[h]:
-                    fetch("scalar", g6[:, t, :], a[t], l6, h)
-            s1 = rows("s1_%d" % h)
-            s2 = rows("s2_%d" % h)
-            o = rows("o%d" % h)
-
-            def larger(first, last):
-                nc.vector.tensor_tensor(o[:, first:last, :], s1[:, first:last, :], s2[:, first:last, :], ALU.max)
-                nc.sync.dma_start(out_rows[:, first:last, cols(h)], o[:, first:last, :])
+                if t in a_n5:
+                    move(False, a_n5[t][:], half_looked_up(a[t], l5, h))
+                if t in a_n6:
+                    move(False, a_n6[t][:], half_looked_up(a[t], l6, h))
+            sum57 = row_sets("sum57_%d" % h, C)
+            sum68 = row_sets("sum68_%d" % h, C)
+            o = row_sets("o%d" % h, C)
 
             for t in range(R):
-                if t >= R - PLAIN_N5[h]:
-                    nc.vector.tensor_tensor(s1[:, t, :], g5[:, t, :], g7[t][:], ALU.add)
-                else:
-                    nc.vector.tensor_tensor(s1[:, t, :], looked_up(a[t], l5, h), g7[t][:], ALU.add)
+                picked = a_n5[t][:] if t in a_n5 else half_looked_up(a[t], l5, h)
+                nc.vector.tensor_tensor(sum57[:, t, :], picked, b_n7[t][:], ALU.add)
                 if t >= 2:
-                    larger((0, 2)[t - 2], t)
-                if t >= R - PLAIN_N6[h]:
-                    nc.vector.tensor_tensor(s2[:, t, :], g6[:, t, :], g8[t][:], ALU.add)
-                else:
-                    nc.vector.tensor_tensor(s2[:, t, :], looked_up(a[t], l6, h), g8[t][:], ALU.add)
-            larger(3, R)
-            o_bf = weave("o%d" % h, o[:], "scalar" if h == 0 else "vector")
+                    done = slice(0, 2) if t == 2 else slice(2, 3)
+                    nc.vector.tensor_tensor(o[:, done, :], sum57[:, done, :], sum68[:, done, :], ALU.max)
+                    nc.sync.dma_start(out_rows[:, done, cols(h)], o[:, done, :])
+                if t < last:
+                    picked = a_n6[t][:] if t in a_n6 else half_looked_up(a[t], l6, h)
+                    nc.vector.tensor_tensor(sum68[:, t, :], picked, b_n8[t][:], ALU.add)
+
+            width = C // (1 + h)
+            parts = [slice(j, j + width) for j in range(0, C, width)]
+            for part in parts:
+                nc.vector.tensor_tensor(sum68[:, last, part], a_n6[last][:, part], b_n8[last][:, part], ALU.add)
+            for part in parts:
+                nc.vector.tensor_tensor(o[:, last, part], sum57[:, last, part], sum68[:, last, part], ALU.max)
+            nc.sync.dma_start(out_rows[:, last, cols(h)], o[:, last, :])
+            o_bf = tile("o_bf%d" % h, [P, C * R], BF16)
             o_codes = tile("o_codes%d" % h, [P, C], U32)
-            nc.vector.quantize_mx(out=o_codes[:].bitcast(FP8X4), scales=o_scales[:, cols(h)], in_=o_bf[:])
+            for part in parts:
+                dst = woven(o_bf[:, R * part.start : R * part.stop])
+                if h == 0:
+                    nc.scalar.copy(dst, planar(o[:, :, part]))
+                else:
+                    nc.vector.tensor_copy(dst, planar(o[:, :, part]))
+            for part in parts:
+                nc.vector.quantize_mx(
+                    out=o_codes[:, part].bitcast(FP8X4),
+                    scales=o_scales[:, h * C + part.start : h * C + part.stop],
+                    in_=o_bf[:, R * part.start : R * part.stop],
+                )
             nc.sync.dma_start(out_words[:, cols(h)], o_codes[:].bitcast(I32))
-        for q in range(4):
+        for q in range(QUADRANTS):
             queue = nc.scalar if q % 2 == 0 else nc.sync
             queue.dma_start(out_2[0, 4 * q : 4 * q + 4, :].bitcast(I32), o_scales[32 * q : 32 * q + 4, :].bitcast(I32))

from contextlib import ExitStack

import concourse.mybir as mybir

F32 = mybir.dt.float32
BF16 = mybir.dt.bfloat16
I32 = mybir.dt.int32
U32 = mybir.dt.uint32
U16 = mybir.dt.uint16
U8 = mybir.dt.uint8
FP8X4 = mybir.dt.float8_e4m3fn_x4
FP4X4 = mybir.dt.float4_e2m1fn_x4
ALU = mybir.AluOpType
ACT = mybir.ActivationFunctionType

P = 128
R = 4
T = 2048
S = 512
C = S // 2
QUADRANTS = 4
PER_COLUMN = 16
PSUM_BANKS = 8

VECTOR_N3 = 2
SCALAR_N6 = 2

FLOPS = 3 * 2 * 512 * 512 * 512


def tile_picked_forkpathboverfdif_none_po_kernel(
    tc, x_words, x_scales, w1_words, w1_scales, gn, w2_words, w2_scales, gm, w3_words, w3_scales,
    offs, n1, n2, n3, n4, n5, n6, n7, n8, out_0, out_1, out_2,
):
    nc = tc.nc
    with ExitStack() as ctx:
        keep = ctx.enter_context(tc.tile_pool(name="keep", bufs=1))
        psum = ctx.enter_context(tc.psum_pool(name="psum", bufs=PSUM_BANKS))

        def tile(name, shape, dtype):
            return keep.tile(shape, dtype, name=name, align_bytes=64)

        def row_sets(name, width):
            return tile(name, [P, R, width], F32)

        def load_list(name, src):
            dst = tile(name, [P, S // PER_COLUMN], U16)
            nc.sync.dma_start(dst[:], src)
            return dst

        def load_words(name, src):
            dst = tile(name, [P, 2 * S], U8)
            nc.sync.dma_start(dst[:].bitcast(I32), src[0].bitcast(I32))
            return dst

        def load_gain(name, src):
            dst = tile(name, [P, R], F32)
            nc.sync.dma_start(dst[:], src.rearrange("(p t) o -> p (t o)", t=R))
            return dst

        def load_scale_rows(dst, src):
            for q in range(QUADRANTS):
                nc.sync.dma_start(dst[32 * q : 32 * q + 4, :].bitcast(I32), src[0, 4 * q : 4 * q + 4, :].bitcast(I32))

        def deal_bytes(name, raw, width):
            dst = tile(name, [P, width * S], U8)
            nc.gpsimd.tensor_copy(
                out=dst[:].rearrange("p (t m b) -> p t m b", t=R, b=width),
                in_=raw[:].rearrange("p (m t b) -> p t m b", t=R, b=width),
            )
            return dst

        def cols(h):
            return slice(h * C, (h + 1) * C)

        def half_looked_up(window, lst, h):
            return window[:].indirect(lst[:, h * C // PER_COLUMN : (h + 1) * C // PER_COLUMN])

        def woven(packed):
            return packed.rearrange("p (c i t) -> p c t i", t=R, i=4)

        def planar(values):
            return values.rearrange("p t (c i) -> p c t i", i=4)

        def weave_times(name, values, gain, width):
            packed = tile(name, [P, width * R], BF16)
            spread = gain[:].unsqueeze(1).unsqueeze(3).to_broadcast([P, width // 4, R, 4])
            nc.vector.tensor_tensor(woven(packed[:]), planar(values), spread, ALU.mult)
            return packed

        def quantise(name, packed, width):
            codes = tile(name + "_codes", [P, width], U32)
            scales = tile(name + "_scales", [P, width], U8)
            nc.vector.quantize_mx(out=codes[:].bitcast(FP8X4), scales=scales[:], in_=packed[:])
            return codes, scales

        def product(acc, words, scales, t, codes, code_scales):
            nc.tensor.matmul_mx(
                out=acc,
                lhsT=words[:, 2 * P * t : 2 * P * (t + 1)].bitcast(FP4X4),
                lhsT_scale=scales[:, P * t : P * (t + 1)],
                rhs=codes.bitcast(FP8X4),
                rhs_scale=code_scales,
                start=True,
                stop=True,
            )

        def move(on_vector, dst, src):
            if on_vector:
                nc.vector.tensor_copy(dst, src)
            else:
                nc.scalar.activation(dst, src, ACT.Copy)

        xs_raw = tile("xs_raw", [P, T], U8)
        w1s_raw = tile("w1s_raw", [P, S], U8)
        w3s_raw = tile("w3s_raw", [P, S], U8)
        w2s_raw = tile("w2s_raw", [P, S], U8)
        y = [tile("y%d" % t, [P, 2 * S], F32) for t in range(R)]
        for raw in (xs_raw, w1s_raw, w3s_raw, w2s_raw):
            nc.gpsimd.memset(raw[:].bitcast(I32), 0)

        offs_t = load_list("offs_t", offs)
        w1w_raw = load_words("w1w_raw", w1_words)
        load_scale_rows(xs_raw, x_scales)
        xw_raw = tile("xw_raw", [P, T], I32)
        nc.sync.dma_start(xw_raw[:], x_words[0].rearrange("p n r -> p (n r)").bitcast(I32))
        load_scale_rows(w1s_raw, w1_scales)
        l3 = load_list("l3", n3)
        l1 = load_list("l1", n1)
        w3w_raw = load_words("w3w_raw", w3_words)
        w2w_raw = load_words("w2w_raw", w2_words)
        l4 = load_list("l4", n4)
        l2 = load_list("l2", n2)
        gm_t = load_gain("gm_t", gm)
        load_scale_rows(w3s_raw, w3_scales)
        load_scale_rows(w2s_raw, w2_scales)
        gn_t = load_gain("gn_t", gn)
        l7 = load_list("l7", n7)
        l8 = load_list("l8", n8)
        l5 = load_list("l5", n5)
        l6 = load_list("l6", n6)

        w1w = tile("w1w", [P, 2 * S], U8)
        nc.scalar.copy(
            out=w1w[:].bitcast(U16).rearrange("p (t c i) -> p c t i", t=R, i=8),
            in_=w1w_raw[:].bitcast(U16).rearrange("p (c i t) -> p c t i", t=R, i=8),
        )
        w1s = deal_bytes("w1s", w1s_raw, 1)
        xs = tile("xs", [P, S], U8)
        nc.vector.tensor_copy(xs[:], xs_raw[:].indirect(offs_t[:]))
        xw = [tile("xw%d" % h, [P, C], U32) for h in range(2)]
        for h in range(2):
            nc.vector.tensor_copy(xw[h][:], half_looked_up(xw_raw[:].bitcast(U32), offs_t, h))
        for t in range(R):
            for h in range(2):
                acc = psum.tile([P, C], F32, name="acc")
                product(acc[:], w1w, w1s, t, xw[h][:], xs[:, cols(h)])
                move(h == 1 and t % 2 == 1, y[t][:, cols(h)], acc[:])

        b = [tile("b%d" % t, [P, S], F32) for t in range(R)]
        a = [tile("a%d" % t, [P, S], F32) for t in range(R)]
        y_n1, y_n2, y_n3, diff, th, prod, z_bare = [
            row_sets(name, S) for name in ("y_n1", "y_n2", "y_n3", "diff", "th", "prod", "z_bare")
        ]
        for t in range(R):
            move(t < VECTOR_N3, y_n3[:, t, :], y[t][:].indirect(l3[:]))
        for t in range(R):
            nc.vector.tensor_tensor(diff[:, t, :], y_n3[:, t, :], y[t][:, :S], ALU.subtract)
            nc.scalar.activation(th[:, t, :], diff[:, t, :], ACT.Tanh)
        for t in range(R):
            nc.vector.tensor_tensor(prod[:, t, :], y[t][:].indirect(l4[:]), th[:, t, :], ALU.mult)
        for t in range(R):
            move(False, y_n1[:, t, :], y[t][:].indirect(l1[:]))
            move(False, y_n2[:, t, :], y[t][:].indirect(l2[:]))

        top = [th[:, 2, :], th[:, 1, :], prod[:, 2, :], prod[:, 3, :]]

        def larger_neighbour(t):
            nc.vector.tensor_tensor(top[t], y_n1[:, t, :], y_n2[:, t, :], ALU.max)

        w3w = deal_bytes("w3w", w3w_raw, 2)
        w3s = deal_bytes("w3s", w3s_raw, 1)
        larger_neighbour(0)
        z2_bf = weave_times("z2_bf", prod[:], gm_t, S)
        larger_neighbour(1)
        z2_codes, z2_scales = quantise("z2", z2_bf, S)
        for t in range(R):
            acc = psum.tile([P, S], F32, name="acc")
            product(acc[:], w3w, w3s, t, z2_codes[:], z2_scales[:])
            move(False, b[t][:], acc[:])
        w2w = deal_bytes("w2w", w2w_raw, 2)

        for t in range(R):
            for part in [slice(0, S)] if t < R - 1 else [cols(0), cols(1)]:
                nc.vector.scalar_tensor_tensor(z_bare[:, t, part], y[t][:, part], -0.75, top[t][:, part], ALU.mult, ALU.add)
            if t + 2 < R:
                larger_neighbour(t + 2)
        w2s = deal_bytes("w2s", w2s_raw, 1)
        z_bf = [weave_times("z_bf%d" % h, z_bare[:, :, cols(h)], gn_t, C) for h in range(2)]
        z_q = [quantise("z%d" % h, z_bf[h], C) for h in range(2)]
        for t in range(R):
            acc = psum.tile([P, S], F32, name="acc")
            for h in range(2):
                product(acc[:, cols(h)], w2w, w2s, t, z_q[h][0][:], z_q[h][1][:])
            move(t == 0, a[t][:], acc[:])

        out_rows = out_0.rearrange("(p t) j -> p t j", t=R)
        out_words = out_1[0].rearrange("p n r -> p (n r)").bitcast(I32)
        o_scales = tile("o_scales", [P, S], U8)
        last = R - 1
        for h in range(2):
            b_n7 = [tile("b_n7_%d" % t, [P, C], F32) for t in range(last)]
            b_n7.append(tile("z_bf0" if h == 0 else "b_n7_last", [P, C], F32))
            b_n8 = [tile("b_n8_%d" % t, [P, C], F32) for t in range(R)]
            for t in range(R):
                move(h == 0 and t == last, b_n7[t][:], half_looked_up(b[t], l7, h))
                move(False, b_n8[t][:], half_looked_up(b[t], l8, h))
            scalar_n5 = [last] if h == 1 else []
            a_n5 = {t: tile("a_n5", [P, C], F32) for t in scalar_n5}
            a_n6 = {t: tile("a_n6_%d_%d" % (h, t), [P, C], F32) for t in range(R - SCALAR_N6, R)}
            for t in range(R):
                if t in a_n5:
                    move(False, a_n5[t][:], half_looked_up(a[t], l5, h))
                if t in a_n6:
                    move(False, a_n6[t][:], half_looked_up(a[t], l6, h))
            sum57 = row_sets("sum57_%d" % h, C)
            sum68 = row_sets("sum68_%d" % h, C)
            o = row_sets("o%d" % h, C)

            for t in range(R):
                picked = a_n5[t][:] if t in a_n5 else half_looked_up(a[t], l5, h)
                nc.vector.tensor_tensor(sum57[:, t, :], picked, b_n7[t][:], ALU.add)
                if t >= 2:
                    done = slice(0, 2) if t == 2 else slice(2, 3)
                    nc.vector.tensor_tensor(o[:, done, :], sum57[:, done, :], sum68[:, done, :], ALU.max)
                    nc.sync.dma_start(out_rows[:, done, cols(h)], o[:, done, :])
                if t < last:
                    picked = a_n6[t][:] if t in a_n6 else half_looked_up(a[t], l6, h)
                    nc.vector.tensor_tensor(sum68[:, t, :], picked, b_n8[t][:], ALU.add)

            width = C // (1 + h)
            parts = [slice(j, j + width) for j in range(0, C, width)]
            for part in parts:
                nc.vector.tensor_tensor(sum68[:, last, part], a_n6[last][:, part], b_n8[last][:, part], ALU.add)
            for part in parts:
                nc.vector.tensor_tensor(o[:, last, part], sum57[:, last, part], sum68[:, last, part], ALU.max)
            nc.sync.dma_start(out_rows[:, last, cols(h)], o[:, last, :])
            o_bf = tile("o_bf%d" % h, [P, C * R], BF16)
            o_codes = tile("o_codes%d" % h, [P, C], U32)
            for part in parts:
                dst = woven(o_bf[:, R * part.start : R * part.stop])
                if h == 0:
                    nc.scalar.copy(dst, planar(o[:, :, part]))
                else:
                    nc.vector.tensor_copy(dst, planar(o[:, :, part]))
            for part in parts:
                nc.vector.quantize_mx(
                    out=o_codes[:, part].bitcast(FP8X4),
                    scales=o_scales[:, h * C + part.start : h * C + part.stop],
                    in_=o_bf[:, R * part.start : R * part.stop],
                )
            nc.sync.dma_start(out_words[:, cols(h)], o_codes[:].bitcast(I32))
        for q in range(QUADRANTS):
            queue = nc.scalar if q % 2 == 0 else nc.sync
            queue.dma_start(out_2[0, 4 * q : 4 * q + 4, :].bitcast(I32), o_scales[32 * q : 32 * q + 4, :].bitcast(I32))
